import numpy as np
import ml_dtypes


def mxq(x, axis, fmt="e4m3"):
    dtype, down = {"e4m3": (ml_dtypes.float8_e4m3fn, 7), "e5m2": (ml_dtypes.float8_e5m2, 14)}[fmt]
    v = np.moveaxis(np.asarray(x, np.float32).astype(ml_dtypes.bfloat16).astype(np.float64), axis, -1)
    blocks = v.reshape(v.shape[:-1] + (-1, 32))
    amax = np.abs(blocks).max(-1, keepdims=True)
    byte = np.maximum(np.where(amax > 0, np.frexp(amax)[1] - 1 + 127, 0) - down, 1)
    scale = np.exp2(byte - 127.0)
    codes = (blocks / scale).astype(np.float32).astype(dtype).astype(np.float64)
    return np.moveaxis((codes * scale).reshape(v.shape), -1, axis)


WIDE = False


def mx_kscale(k):
    if not WIDE:
        return np.ones(k)
    levels = np.array([10, -10, 5, -5, 0])
    if k % 512:
        return np.exp2(np.random.permutation(np.resize(levels, k // 32))).repeat(32)
    a = np.empty((k // 512, 16))
    for p in range(k // 512):
        a[p, :8] = np.random.permutation(np.resize(levels, 8))
        for g in range(8):
            far = levels[np.abs(levels - a[p, g]) >= 10]
            a[p, g + 8] = far[np.random.randint(len(far))]
    return np.exp2(a.ravel()).repeat(32)


def f64(x):
    return np.asarray(x).astype(np.float64)


def striped(idx):
    return np.tile(idx.reshape(-1, 16).T, (8, 1)).astype(np.uint16)


def unstriped(offs):
    return offs[:16].T.reshape(-1).astype(np.int64)


def striped8(idx):
    return np.concatenate([x.reshape(-1, 16).T for x in idx]).astype(np.uint16)


def runs(offs, k):
    lists = np.stack([offs[16 * r : 16 * r + 16].T.reshape(-1) for r in range(8)]).astype(np.int64)
    return lists[np.arange(k) % 512 // 64]


def pack_weight(w):
    k, n = w.shape
    w = f64(np.asarray(w, np.float32).astype(ml_dtypes.bfloat16)).reshape(k // 32, 32, n)
    amax = np.abs(w).max(1)
    byte = np.clip(np.where(amax > 0, np.frexp(amax)[1] - 1 + 127 - 7, 1), 1, 254)
    scaled = (w * np.exp2(127.0 - byte)[:, None, :]).reshape(k, n).astype(np.float32)
    words = np.ascontiguousarray(scaled.reshape(k // 512, 128, 4, n).transpose(0, 1, 3, 2)).astype(ml_dtypes.float8_e4m3fn).view(np.uint8)
    return words, np.ascontiguousarray(byte.astype(np.uint8).reshape(k // 512, 16, n))


def unpack_weight(words, scales):
    g, p, n, _ = words.shape
    vals = np.ascontiguousarray(words).view(ml_dtypes.float8_e4m3fn).astype(np.float64) * np.repeat(np.exp2(scales.astype(np.float64) - 127.0), 8, axis=1)[..., None]
    return vals.transpose(0, 1, 3, 2).reshape(g * 512, n)


def sigmoid(v):
    return 1.0 / (1.0 + np.exp(-np.maximum(v, -700.0)))

def planes(y):
    n, m = y.shape
    v = y.astype(np.float32).astype(ml_dtypes.bfloat16).astype(np.float64).reshape(n // 32, 32, m)
    top = np.abs(v).max(1)
    byte = np.clip(np.where(top > 0, np.frexp(top)[1] - 1 + 127 - 7, 1), 1, 254)
    codes = (v * np.exp2(127.0 - byte)[:, None, :]).reshape(n, m).astype(np.float32).astype(ml_dtypes.float8_e4m3fn).view(np.uint8)
    words = codes.reshape(n // 512, 128, 4, m).transpose(0, 1, 3, 2)
    return np.ascontiguousarray(words), np.ascontiguousarray(byte.astype(np.uint8).reshape(n // 512, 16, m))


K, T, S, N, H = 512, 2048, 512, 512, 512


def setup_inputs():
    n = np.random.standard_normal
    s = mx_kscale(K)[:, None]
    u = mx_kscale(H)
    packed_xT = pack_weight(n((K, T)) * s)
    packed_w1 = pack_weight(n((K, H)) / np.sqrt(K) / s)
    packed_w2 = pack_weight(n((H, N)) / np.sqrt(H) / u[:, None])
    return {
        "x_words": packed_xT[0],
        "x_scales": packed_xT[1],
        "w1_words": packed_w1[0],
        "w1_scales": packed_w1[1],
        "gn": (np.random.uniform(0.5, 1.5, (H, 1)) * u[:, None]).astype(np.float32),
        "w2_words": packed_w2[0],
        "w2_scales": packed_w2[1],
        "offs": striped(np.random.permutation(T)[:S]),
        "n1": striped8(np.stack([np.random.permutation(S) for _ in range(8)])),
        "n2": striped8(np.stack([np.random.permutation(S) for _ in range(8)])),
        "n3": striped8(np.stack([np.random.permutation(S) for _ in range(8)])),
        "n4": striped8(np.stack([np.random.permutation(S) for _ in range(8)])),
        "n5": striped8(np.stack([np.random.permutation(S) for _ in range(8)])),
        "n6": striped8(np.stack([np.random.permutation(S) for _ in range(8)])),
    }


def reference(x_words, x_scales, w1_words, w1_scales, gn, w2_words, w2_scales, offs, n1, n2, n3, n4, n5, n6):
    xq = unpack_weight(x_words, x_scales)[:, unstriped(offs)]
    y = unpack_weight(w1_words, w1_scales).T @ xq
    pa = y[np.arange(H)[:, None], runs(n1, H)]
    z = f64(gn) * (pa + (sigmoid(y[np.arange(H)[:, None], runs(n2, H)])) * (y[np.arange(H)[:, None], runs(n3, H)] - pa))
    h = unpack_weight(w2_words, w2_scales).T @ mxq(z, 0, "e4m3")
    out_0 = y * (h[np.arange(N)[:, None], runs(n4, N)] - h) + 0.5 * ((y[np.arange(H)[:, None], runs(n6, H)]) * (h[np.arange(N)[:, None], runs(n5, N)] - h))
    return (out_0,) + planes(out_0)

@@ -1,0 +1,183 @@
+from contextlib import ExitStack
+
+import concourse.mybir as mybir
+
+F32 = mybir.dt.float32
+BF16 = mybir.dt.bfloat16
+I32 = mybir.dt.int32
+U32 = mybir.dt.uint32
+U16 = mybir.dt.uint16
+U8 = mybir.dt.uint8
+FP8X4 = mybir.dt.float8_e4m3fn_x4
+ALU = mybir.AluOpType
+ACT = mybir.ActivationFunctionType
+
+P = 128
+PACK = 4
+T = 2048
+S = 512
+H = 512
+FLOPS = 2 * 2 * 512 * 512 * 512
+Z_CHUNKS = [(0, 256), (256, 512)]
+OUT_CHUNKS = [(0, 256), (256, 384), (384, 512)]
+EARLY = (0, 1)
+
+
+def words_view(dram):
+    return dram[0].rearrange("p n t -> p (n t)").bitcast(I32)
+
+
+def tile_picked_skipflowblerp_none_po_kernel(
+    tc, x_words, x_scales, w1_words, w1_scales, gn, w2_words, w2_scales, offs, n1, n2, n3, n4, n5, n6, out_0, out_1, out_2
+):
+    nc = tc.nc
+    with ExitStack() as ctx:
+        keep = ctx.enter_context(tc.tile_pool(name="keep", bufs=1))
+        psum = ctx.enter_context(tc.psum_pool(name="psum", bufs=1))
+
+        def load_list(name, dram):
+            tile = keep.tile([P, S // 16], U16, name=name)
+            nc.sync.dma_start(tile[:], dram)
+            return tile
+
+        def entries(tile, lo, hi):
+            return tile[:, lo // 16 : hi // 16]
+
+        def load_scales(name, dram, width, clear, queue):
+            tile = keep.tile([P, width], U8, name=name, align_bytes=64)
+            clear.memset(tile[:].bitcast(I32), 0)
+            for q in range(4):
+                queue.dma_start(tile[32 * q : 32 * q + 4, :].bitcast(I32), dram[0, 4 * q : 4 * q + 4, :].bitcast(I32))
+            return tile
+
+        def load_words(name, dram, width):
+            tile = keep.tile([P, width], I32, name=name, align_bytes=64)
+            nc.sync.dma_start(tile[:], words_view(dram))
+            return tile
+
+        def deal(name, words, scales):
+            dealt_words = keep.tile([P, H], U32, name=name + "_dw", align_bytes=64)
+            dealt_scales = keep.tile([P, H], U8, name=name + "_ds", align_bytes=64)
+            nc.vector.tensor_copy(
+                dealt_words[:].rearrange("p (t m) -> p m t", t=PACK),
+                words[:].bitcast(U32).rearrange("p (m t) -> p m t", t=PACK),
+            )
+            nc.vector.tensor_copy(
+                dealt_scales[:].rearrange("p (t m) -> p t m", t=PACK),
+                scales[:].rearrange("p (m t) -> p t m", t=PACK),
+            )
+            return dealt_words, dealt_scales
+
+        warm_in = keep.tile([P, 1], F32, name="warm_in")
+        warm_out = keep.tile([P, 1], F32, name="warm_out")
+        nc.vector.memset(warm_in[:], 0.0)
+        nc.scalar.activation(warm_out[:], warm_in[:], ACT.Sigmoid)
+
+        w1w = load_words("w1w", w1_words, H)
+        offs_t = load_list("offs_t", offs)
+        xs = load_scales("xs", x_scales, T, nc.gpsimd, nc.sync)
+        xw = load_words("xw", x_words, T)
+        w1s = load_scales("w1s", w1_scales, H, nc.gpsimd, nc.scalar)
+        n2_t = load_list("n2_t", n2)
+        gn_t = keep.tile([P, PACK], F32, name="gn_t")
+        nc.sync.dma_start(gn_t[:], gn.rearrange("(p t) o -> p (t o)", t=PACK))
+        n6_t = load_list("n6_t", n6)
+        n3_t = load_list("n3_t", n3)
+        n1_t = load_list("n1_t", n1)
+        w2w = load_words("w2w", w2_words, H)
+        w2s = load_scales("w2s", w2_scales, H, nc.gpsimd, nc.sync)
+        n4_t = load_list("n4_t", n4)
+        n5_t = load_list("n5_t", n5)
+
+        w1dw, w1ds = deal("w1", w1w, w1s)
+        xgs = keep.tile([P, S], U8, name="xgs", align_bytes=64)
+        xgw = keep.tile([P, S], U32, name="xgw", align_bytes=64)
+        nc.vector.tensor_copy(xgs[:], xs[:].indirect(offs_t[:]))
+        nc.vector.tensor_copy(xgw[:], xw[:].bitcast(U32).indirect(offs_t[:]))
+        neg_gn = keep.tile([P, PACK], F32, name="neg_gn")
+        nc.vector.tensor_scalar(neg_gn[:], gn_t[:], -1.0, None, ALU.mult)
+
+        y_ps = [psum.tile([P, S], F32, name="y_ps%d" % t) for t in range(PACK)]
+        h_ps = [psum.tile([P, S], F32, name="h_ps%d" % t) for t in range(PACK)]
+        for t in range(PACK):
+            cols = slice(t * P, (t + 1) * P)
+            nc.tensor.matmul_mx(
+                y_ps[t][:], lhsT=w1dw[:, cols].bitcast(FP8X4), lhsT_scale=w1ds[:, cols],
+                rhs=xgw[:].bitcast(FP8X4), rhs_scale=xgs[:], start=True, stop=True,
+            )
+        w2dw, w2ds = deal("w2", w2w, w2s)
+
+        y = [keep.tile([P, S], F32, name="y%d" % t) for t in range(PACK)]
+        y6 = keep.tile([P, len(EARLY), S], F32, name="y6")
+        zw = keep.tile([P, S], U32, name="zw", align_bytes=64)
+        zs = keep.tile([P, S], U8, name="zs", align_bytes=64)
+        for c, (lo, hi) in enumerate(Z_CHUNKS):
+            n = hi - lo
+            a = keep.tile([P, PACK, n], F32, name="a%d" % c)
+            b = keep.tile([P, PACK, n], F32, name="b%d" % c)
+            for t in range(PACK):
+                if c == 0:
+                    nc.scalar.copy(y[t][:], y_ps[t][:])
+                s = keep.tile([P, n], F32, name="s%d_%d" % (c, t))
+                sg = keep.tile([P, n], F32, name="sg%d_%d" % (c, t))
+                qg = keep.tile([P, n], F32, name="qg%d_%d" % (c, t))
+                nc.scalar.activation(s[:], y[t][:].indirect(entries(n2_t, lo, hi)), ACT.Sigmoid)
+                nc.scalar.activation(sg[:], s[:], ACT.Identity, scale=gn_t[:, t : t + 1])
+                nc.scalar.activation(qg[:], s[:], ACT.Identity, scale=neg_gn[:, t : t + 1], bias=gn_t[:, t : t + 1])
+                nc.vector.tensor_tensor(b[:, t, :], y[t][:].indirect(entries(n3_t, lo, hi)), sg[:], ALU.mult)
+                nc.vector.tensor_tensor(a[:, t, :], y[t][:].indirect(entries(n1_t, lo, hi)), qg[:], ALU.mult)
+            zb = keep.tile([P, n, PACK], BF16, name="zb%d" % c, align_bytes=64)
+            nc.vector.tensor_tensor(
+                zb[:].rearrange("p (c i) t -> p c t i", i=2),
+                a[:].rearrange("p t (c i) -> p c t i", i=2),
+                b[:].rearrange("p t (c i) -> p c t i", i=2),
+                ALU.add,
+            )
+            nc.vector.quantize_mx(zw[:, lo:hi].bitcast(FP8X4), zs[:, lo:hi], zb[:].rearrange("p n t -> p (n t)"))
+            for t in range(PACK):
+                cols = slice(t * P, (t + 1) * P)
+                nc.tensor.matmul_mx(
+                    h_ps[t][:, lo:hi], lhsT=w2dw[:, cols].bitcast(FP8X4), lhsT_scale=w2ds[:, cols],
+                    rhs=zw[:, lo:hi].bitcast(FP8X4), rhs_scale=zs[:, lo:hi], start=True, stop=True,
+                )
+        for t in EARLY:
+            for lo, hi in Z_CHUNKS:
+                nc.vector.tensor_copy(y6[:, t, lo:hi], y[t][:].indirect(entries(n6_t, lo, hi)))
+
+        h = [keep.tile([P, S], F32, name="h%d" % t) for t in range(PACK)]
+        hc = keep.tile([P, PACK, S], F32, name="hc")
+        ow = keep.tile([P, S], U32, name="ow", align_bytes=64)
+        osc = keep.tile([P, S], U8, name="osc", align_bytes=64)
+        out_rows = out_0.rearrange("(p t) j -> p t j", t=PACK)
+        for c, (lo, hi) in enumerate(OUT_CHUNKS):
+            n = hi - lo
+            d4 = keep.tile([P, PACK, n], F32, name="d4_%d" % c)
+            d5 = keep.tile([P, PACK, n], F32, name="d5_%d" % c)
+            u = keep.tile([P, PACK, n], F32, name="u%d" % c)
+            v = keep.tile([P, PACK, n], F32, name="v%d" % c)
+            o = keep.tile([P, PACK, n], F32, name="o%d" % c)
+            for t in range(PACK):
+                if c == 0:
+                    nc.scalar.copy(h[t][:], h_ps[t][:])
+                    nc.scalar.copy(hc[:, t, :], h_ps[t][:])
+                nc.vector.tensor_tensor(d4[:, t, :], h[t][:].indirect(entries(n4_t, lo, hi)), hc[:, t, lo:hi], ALU.subtract)
+                nc.vector.tensor_tensor(d5[:, t, :], h[t][:].indirect(entries(n5_t, lo, hi)), hc[:, t, lo:hi], ALU.subtract)
+                nc.vector.tensor_tensor(u[:, t, :], d4[:, t, :], y[t][:, lo:hi], ALU.mult)
+                if t in EARLY:
+                    nc.vector.tensor_tensor(v[:, t, :], d5[:, t, :], y6[:, t, lo:hi], ALU.mult)
+                else:
+                    nc.vector.tensor_tensor(v[:, t, :], y[t][:].indirect(entries(n6_t, lo, hi)), d5[:, t, :], ALU.mult)
+            nc.vector.scalar_tensor_tensor(o[:], v[:], 0.5, u[:], ALU.mult, ALU.add)
+            nc.sync.dma_start(out_rows[:, :, lo:hi], o[:])
+            ob = keep.tile([P, n, PACK], BF16, name="ob%d" % c, align_bytes=64)
+            grouped = ob[:].rearrange("p (c i) t -> p c t i", i=2)
+            source = o[:].rearrange("p t (c i) -> p c t i", i=2)
+            if c == len(OUT_CHUNKS) - 1:
+                nc.vector.tensor_copy(grouped, source)
+            else:
+                nc.scalar.copy(grouped, source)
+            nc.vector.quantize_mx(ow[:, lo:hi].bitcast(FP8X4), osc[:, lo:hi], ob[:].rearrange("p n t -> p (n t)"))
+            nc.sync.dma_start(words_view(out_1)[:, lo:hi], ow[:, lo:hi].bitcast(I32))
+        for q in range(4):
+            queue = nc.scalar if q % 2 else nc.sync
+            queue.dma_start(out_2[0, 4 * q : 4 * q + 4, :].bitcast(I32), osc[32 * q : 32 * q + 4, :].bitcast(I32))

@@ -1,6 +1,7 @@
 from contextlib import ExitStack
 
 import concourse.mybir as mybir
+from concourse.masks import make_identity
 
 F32 = mybir.dt.float32
 BF16 = mybir.dt.bfloat16
@@ -18,9 +19,11 @@ T = 2048
 S = 512
 H = 512
 FLOPS = 2 * 2 * 512 * 512 * 512
-Z_CHUNKS = [(0, 256), (256, 512)]
+Z_CHUNKS = [(0, 512)]
 OUT_CHUNKS = [(0, 256), (256, 384), (384, 512)]
-EARLY = (0, 1)
+EARLY = (0,)
+LATE = (1, 2)
+XW_FIRST = 512
 
 
 def words_view(dram):
@@ -44,20 +47,20 @@ def tile_picked_skipflowblerp_none_po_kernel(
             return tile[:, lo // 16 : hi // 16]
 
         def load_scales(name, dram, width, clear, queue):
-            tile = keep.tile([P, width], U8, name=name, align_bytes=64)
+            tile = keep.tile([P, width], U8, name=name, tag=name, align_bytes=64)
             clear.memset(tile[:].bitcast(I32), 0)
             for q in range(4):
                 queue.dma_start(tile[32 * q : 32 * q + 4, :].bitcast(I32), dram[0, 4 * q : 4 * q + 4, :].bitcast(I32))
             return tile
 
         def load_words(name, dram, width):
-            tile = keep.tile([P, width], I32, name=name, align_bytes=64)
+            tile = keep.tile([P, width], I32, name=name, tag=name, align_bytes=64)
             nc.sync.dma_start(tile[:], words_view(dram))
             return tile
 
         def deal(name, words, scales):
-            dealt_words = keep.tile([P, H], U32, name=name + "_dw", align_bytes=64)
-            dealt_scales = keep.tile([P, H], U8, name=name + "_ds", align_bytes=64)
+            dealt_words = keep.tile([P, H], U32, name=name + "_dw", tag="w1w", align_bytes=64)
+            dealt_scales = keep.tile([P, H], U8, name=name + "_ds", tag="w1s", align_bytes=64)
             nc.vector.tensor_copy(
                 dealt_words[:].rearrange("p (t m) -> p m t", t=PACK),
                 words[:].bitcast(U32).rearrange("p (m t) -> p m t", t=PACK),
@@ -68,28 +71,29 @@ def tile_picked_skipflowblerp_none_po_kernel(
             )
             return dealt_words, dealt_scales
 
+        xw = keep.tile([P, T], I32, name="xw", align_bytes=64)
+        nc.sync.dma_start(xw[:, :XW_FIRST], words_view(x_words)[:, :XW_FIRST])
+        xs = load_scales("xs", x_scales, T, nc.vector, nc.sync)
+        offs_t = load_list("offs_t", offs)
+        nc.sync.dma_start(xw[:, XW_FIRST:], words_view(x_words)[:, XW_FIRST:])
         warm_in = keep.tile([P, 1], F32, name="warm_in")
         warm_out = keep.tile([P, 1], F32, name="warm_out")
         nc.vector.memset(warm_in[:], 0.0)
         nc.scalar.activation(warm_out[:], warm_in[:], ACT.Sigmoid)
 
         w1w = load_words("w1w", w1_words, H)
-        offs_t = load_list("offs_t", offs)
-        xs = load_scales("xs", x_scales, T, nc.gpsimd, nc.sync)
-        xw = load_words("xw", x_words, T)
-        w1s = load_scales("w1s", w1_scales, H, nc.gpsimd, nc.scalar)
+        w1s = load_scales("w1s", w1_scales, H, nc.gpsimd, nc.sync)
         n2_t = load_list("n2_t", n2)
         gn_t = keep.tile([P, PACK], F32, name="gn_t")
         nc.sync.dma_start(gn_t[:], gn.rearrange("(p t) o -> p (t o)", t=PACK))
         n6_t = load_list("n6_t", n6)
-        n3_t = load_list("n3_t", n3)
-        n1_t = load_list("n1_t", n1)
         w2w = load_words("w2w", w2_words, H)
         w2s = load_scales("w2s", w2_scales, H, nc.gpsimd, nc.sync)
+        n3_t = load_list("n3_t", n3)
+        n1_t = load_list("n1_t", n1)
         n4_t = load_list("n4_t", n4)
         n5_t = load_list("n5_t", n5)
 
-        w1dw, w1ds = deal("w1", w1w, w1s)
         xgs = keep.tile([P, S], U8, name="xgs", align_bytes=64)
         xgw = keep.tile([P, S], U32, name="xgw", align_bytes=64)
         nc.vector.tensor_copy(xgs[:], xs[:].indirect(offs_t[:]))
@@ -100,37 +104,47 @@ def tile_picked_skipflowblerp_none_po_kernel(
         y_ps = [psum.tile([P, S], F32, name="y_ps%d" % t) for t in range(PACK)]
         h_ps = [psum.tile([P, S], F32, name="h_ps%d" % t) for t in range(PACK)]
         for t in range(PACK):
-            cols = slice(t * P, (t + 1) * P)
+            w1dw = keep.tile([P, P], U32, name="w1dw%d" % t, align_bytes=64)
+            w1ds = keep.tile([P, P], U8, name="w1ds%d" % t, align_bytes=64)
+            nc.vector.tensor_copy(w1dw[:], w1w[:].bitcast(U32)[:, t::PACK])
+            nc.vector.tensor_copy(w1ds[:], w1s[:, t::PACK])
             nc.tensor.matmul_mx(
-                y_ps[t][:], lhsT=w1dw[:, cols].bitcast(FP8X4), lhsT_scale=w1ds[:, cols],
+                y_ps[t][:], lhsT=w1dw[:].bitcast(FP8X4), lhsT_scale=w1ds[:],
                 rhs=xgw[:].bitcast(FP8X4), rhs_scale=xgs[:], start=True, stop=True,
             )
         w2dw, w2ds = deal("w2", w2w, w2s)
 
-        y = [keep.tile([P, S], F32, name="y%d" % t) for t in range(PACK)]
-        y6 = keep.tile([P, len(EARLY), S], F32, name="y6")
+        y = [keep.tile([P, 2 * S], F32, name="y%d" % t) for t in range(PACK)]
+        for t in range(PACK):
+            nc.gpsimd.memset(y[t][:, S:], 0.0)
+        ident = keep.tile([P, P], F32, name="ident")
+        make_identity(nc, ident[:])
+        h = [keep.tile([P, S], F32, name="h%d" % t) for t in range(PACK)]
+        hc = [keep.tile([P, S], F32, name="hc%d" % t) for t in range(PACK)]
         zw = keep.tile([P, S], U32, name="zw", align_bytes=64)
         zs = keep.tile([P, S], U8, name="zs", align_bytes=64)
-        for c, (lo, hi) in enumerate(Z_CHUNKS):
+        shared = keep.tile([P, len(EARLY) + PACK, S], F32, name="shared")
+        y6 = shared[:, :PACK, :]
+        a = shared[:, len(EARLY) :, :]
+        b = keep.tile([P, PACK, S], F32, name="b", tag="w2w", align_bytes=64)
+
+        def blend(t, lo, hi):
             n = hi - lo
-            a = keep.tile([P, PACK, n], F32, name="a%d" % c)
-            b = keep.tile([P, PACK, n], F32, name="b%d" % c)
-            for t in range(PACK):
-                if c == 0:
-                    nc.scalar.copy(y[t][:], y_ps[t][:])
-                s = keep.tile([P, n], F32, name="s%d_%d" % (c, t))
-                sg = keep.tile([P, n], F32, name="sg%d_%d" % (c, t))
-                qg = keep.tile([P, n], F32, name="qg%d_%d" % (c, t))
-                nc.scalar.activation(s[:], y[t][:].indirect(entries(n2_t, lo, hi)), ACT.Sigmoid)
-                nc.scalar.activation(sg[:], s[:], ACT.Identity, scale=gn_t[:, t : t + 1])
-                nc.scalar.activation(qg[:], s[:], ACT.Identity, scale=neg_gn[:, t : t + 1], bias=gn_t[:, t : t + 1])
-                nc.vector.tensor_tensor(b[:, t, :], y[t][:].indirect(entries(n3_t, lo, hi)), sg[:], ALU.mult)
-                nc.vector.tensor_tensor(a[:, t, :], y[t][:].indirect(entries(n1_t, lo, hi)), qg[:], ALU.mult)
-            zb = keep.tile([P, n, PACK], BF16, name="zb%d" % c, align_bytes=64)
+            s = keep.tile([P, n], F32, name="s%d_%d" % (lo, t), tag="s%d_%d" % (lo, t))
+            sg = keep.tile([P, n], F32, name="sg%d_%d" % (lo, t), tag="w2s" if t == 1 else "sg%d_%d" % (lo, t), align_bytes=64)
+            qg = keep.tile([P, n], F32, name="qg%d_%d" % (lo, t))
+            nc.scalar.activation(s[:], y[t][:].indirect(entries(n2_t, lo, hi)), ACT.Sigmoid)
+            nc.scalar.activation(sg[:], s[:], ACT.Identity, scale=gn_t[:, t : t + 1])
+            nc.vector.tensor_scalar(qg[:], s[:], neg_gn[:, t : t + 1], gn_t[:, t : t + 1], ALU.mult, ALU.add)
+            nc.vector.tensor_tensor(b[:, t, lo:hi], y[t][:].indirect(entries(n3_t, lo, hi)), sg[:], ALU.mult)
+            nc.vector.tensor_tensor(a[:, t, lo:hi], y[t][:].indirect(entries(n1_t, lo, hi)), qg[:], ALU.mult)
+
+        def second_product(lo, hi):
+            zb = keep.tile([P, hi - lo, PACK], BF16, name="zb%d" % lo, align_bytes=64)
             nc.vector.tensor_tensor(
                 zb[:].rearrange("p (c i) t -> p c t i", i=2),
-                a[:].rearrange("p t (c i) -> p c t i", i=2),
-                b[:].rearrange("p t (c i) -> p c t i", i=2),
+                a[:, :, lo:hi].rearrange("p t (c i) -> p c t i", i=2),
+                b[:, :, lo:hi].rearrange("p t (c i) -> p c t i", i=2),
                 ALU.add,
             )
             nc.vector.quantize_mx(zw[:, lo:hi].bitcast(FP8X4), zs[:, lo:hi], zb[:].rearrange("p n t -> p (n t)"))
@@ -140,44 +154,98 @@ def tile_picked_skipflowblerp_none_po_kernel(
                     h_ps[t][:, lo:hi], lhsT=w2dw[:, cols].bitcast(FP8X4), lhsT_scale=w2ds[:, cols],
                     rhs=zw[:, lo:hi].bitcast(FP8X4), rhs_scale=zs[:, lo:hi], start=True, stop=True,
                 )
-        for t in EARLY:
-            for lo, hi in Z_CHUNKS:
-                nc.vector.tensor_copy(y6[:, t, lo:hi], y[t][:].indirect(entries(n6_t, lo, hi)))
 
-        h = [keep.tile([P, S], F32, name="h%d" % t) for t in range(PACK)]
-        hc = keep.tile([P, PACK, S], F32, name="hc")
+        for t in range(PACK):
+            nc.scalar.copy(y[t][:, :S], y_ps[t][:])
+            blend(t, 0, S)
+        second_product(0, S)
+        for t in range(PACK):
+            nc.scalar.copy(h[t][:], h_ps[t][:])
+            nc.scalar.copy(hc[t][:], h_ps[t][:])
+        y_all = keep.tile([P, PACK, S], F32, name="y_all", tag="s0_3")
+        for t in range(PACK):
+            nc.scalar.copy(y_all[:, t, :], y_ps[t][:])
+
+        fetched = len(EARLY + LATE)
+        for t in EARLY + LATE:
+            nc.vector.tensor_copy(y6[:, t, :], y[t][:].indirect(n6_t[:]))
+
         ow = keep.tile([P, S], U32, name="ow", align_bytes=64)
         osc = keep.tile([P, S], U8, name="osc", align_bytes=64)
         out_rows = out_0.rearrange("(p t) j -> p t j", t=PACK)
-        for c, (lo, hi) in enumerate(OUT_CHUNKS):
-            n = hi - lo
-            d4 = keep.tile([P, PACK, n], F32, name="d4_%d" % c)
-            d5 = keep.tile([P, PACK, n], F32, name="d5_%d" % c)
-            u = keep.tile([P, PACK, n], F32, name="u%d" % c)
-            v = keep.tile([P, PACK, n], F32, name="v%d" % c)
-            o = keep.tile([P, PACK, n], F32, name="o%d" % c)
+        parts = {}
+        last = len(OUT_CHUNKS) - 1
+
+        def differences(c, t):
+            lo, hi = OUT_CHUNKS[c]
+            if t == 0:
+                parts[c] = [
+                    keep.tile([P, PACK, hi - lo], F32, name="%s_%d" % (nm, c), tag=nm if nm[0] == "d" else "%s_%d" % (nm, c))
+                    for nm in ("d4", "d5", "u", "v")
+                ]
+            d4, d5, u, v = parts[c]
+            nc.vector.tensor_tensor(d5[:, t, :], h[t][:].indirect(entries(n5_t, lo, hi)), hc[t][:, lo:hi], ALU.subtract)
+            nc.vector.tensor_tensor(d4[:, t, :], h[t][:].indirect(entries(n4_t, lo, hi)), hc[t][:, lo:hi], ALU.subtract)
+
+        def products(c):
+            lo, hi = OUT_CHUNKS[c]
+            d4, d5, u, v = parts[c]
+            nc.vector.tensor_tensor(v[:, :fetched, :], d5[:, :fetched, :], y6[:, :fetched, lo:hi], ALU.mult)
+            for t in range(fetched, PACK):
+                nc.vector.tensor_tensor(v[:, t, :], y[t][:].indirect(entries(n6_t, lo, hi)), d5[:, t, :], ALU.mult)
+            nc.vector.scalar_tensor_tensor(u[:], d4[:], 1.0 if c == last else 2.0, y_all[:, :, lo:hi], ALU.mult, ALU.mult)
+
+        def sum_on_tensor(c, lo):
+            d4, d5, u, v = parts[c]
+            block = lo // P
+            at = slice(lo - OUT_CHUNKS[c][0], lo - OUT_CHUNKS[c][0] + P)
+            turned_ps, back_ps = y_ps[2 * (block % 2)], y_ps[2 * (block % 2) + 1]
             for t in range(PACK):
-                if c == 0:
-                    nc.scalar.copy(h[t][:], h_ps[t][:])
-                    nc.scalar.copy(hc[:, t, :], h_ps[t][:])
-                nc.vector.tensor_tensor(d4[:, t, :], h[t][:].indirect(entries(n4_t, lo, hi)), hc[:, t, lo:hi], ALU.subtract)
-                nc.vector.tensor_tensor(d5[:, t, :], h[t][:].indirect(entries(n5_t, lo, hi)), hc[:, t, lo:hi], ALU.subtract)
-                nc.vector.tensor_tensor(u[:, t, :], d4[:, t, :], y[t][:, lo:hi], ALU.mult)
-                if t in EARLY:
-                    nc.vector.tensor_tensor(v[:, t, :], d5[:, t, :], y6[:, t, lo:hi], ALU.mult)
-                else:
-                    nc.vector.tensor_tensor(v[:, t, :], y[t][:].indirect(entries(n6_t, lo, hi)), d5[:, t, :], ALU.mult)
+                cols = slice(t * P, (t + 1) * P)
+                nc.tensor.matmul(turned_ps[:, cols], u[:, t, at], ident[:], is_transpose=True, start=True, stop=False)
+                nc.tensor.matmul(turned_ps[:, cols], v[:, t, at], ident[:], is_transpose=True, start=False, stop=True)
+            turned = keep.tile([P, S], F32, name="turned%d" % block)
+            nc.scalar.activation(turned[:], turned_ps[:], ACT.Copy, scale=0.5)
+            for t in range(PACK):
+                cols = slice(t * P, (t + 1) * P)
+                nc.tensor.transpose(back_ps[:, cols], turned[:, cols], ident[:])
+            o = keep.tile([P, PACK, P], F32, name="o%d" % block)
+            ob = keep.tile([P, P, PACK], BF16, name="ob%d" % block, align_bytes=64)
+            nc.scalar.copy(o[:], back_ps[:].rearrange("p (t j) -> p t j", t=PACK))
+            nc.sync.dma_start(out_rows[:, :, lo : lo + P], o[:])
+            nc.scalar.copy(ob[:], back_ps[:].rearrange("p (t j) -> p j t", t=PACK))
+            return ob
+
+        def sum_on_vector(c):
+            lo, hi = OUT_CHUNKS[c]
+            d4, d5, u, v = parts[c]
+            o = keep.tile([P, PACK, P], F32, name="o_last")
+            ob = keep.tile([P, P, PACK], BF16, name="ob_last", align_bytes=64)
             nc.vector.scalar_tensor_tensor(o[:], v[:], 0.5, u[:], ALU.mult, ALU.add)
             nc.sync.dma_start(out_rows[:, :, lo:hi], o[:])
-            ob = keep.tile([P, n, PACK], BF16, name="ob%d" % c, align_bytes=64)
-            grouped = ob[:].rearrange("p (c i) t -> p c t i", i=2)
-            source = o[:].rearrange("p t (c i) -> p c t i", i=2)
-            if c == len(OUT_CHUNKS) - 1:
-                nc.vector.tensor_copy(grouped, source)
-            else:
-                nc.scalar.copy(grouped, source)
-            nc.vector.quantize_mx(ow[:, lo:hi].bitcast(FP8X4), osc[:, lo:hi], ob[:].rearrange("p n t -> p (n t)"))
-            nc.sync.dma_start(words_view(out_1)[:, lo:hi], ow[:, lo:hi].bitcast(I32))
+            planes(2 * P, rounded[2 * P])
+            nc.vector.tensor_copy(ob[:].rearrange("p (c i) t -> p c t i", i=2), o[:].rearrange("p t (c i) -> p c t i", i=2))
+            return ob
+
+        def planes(lo, ob):
+            nc.vector.quantize_mx(ow[:, lo : lo + P].bitcast(FP8X4), osc[:, lo : lo + P], ob[:].rearrange("p n t -> p (n t)"))
+            if lo % (2 * P):
+                nc.sync.dma_start(words_view(out_1)[:, lo - P : lo + P], ow[:, lo - P : lo + P].bitcast(I32))
+
+        rounded = {}
+        for t in range(PACK):
+            differences(0, t)
+        for c in range(last):
+            products(c)
+            for lo in range(OUT_CHUNKS[c][0], OUT_CHUNKS[c][1], P):
+                rounded[lo] = sum_on_tensor(c, lo)
+            for t in range(PACK):
+                differences(c + 1, t)
+        planes(0, rounded[0])
+        products(last)
+        planes(P, rounded[P])
+        rounded[3 * P] = sum_on_vector(last)
+        planes(3 * P, rounded[3 * P])
         for q in range(4):
             queue = nc.scalar if q % 2 else nc.sync
             queue.dma_start(out_2[0, 4 * q : 4 * q + 4, :].bitcast(I32), osc[32 * q : 32 * q + 4, :].bitcast(I32))

@@ -20,10 +20,11 @@ S = 512
 H = 512
 FLOPS = 2 * 2 * 512 * 512 * 512
 Z_CHUNKS = [(0, 512)]
-OUT_CHUNKS = [(0, 256), (256, 384), (384, 512)]
-EARLY = (0,)
-LATE = (1, 2)
+OUT_CHUNKS = [(0, 256), (256, 512)]
+EARLY = (0, 1)
+LATE = (2, 3)
 XW_FIRST = 512
+SCALAR_COLS = 80
 
 
 def words_view(dram):
@@ -87,10 +88,12 @@ def tile_picked_skipflowblerp_none_po_kernel(
         gn_t = keep.tile([P, PACK], F32, name="gn_t")
         nc.sync.dma_start(gn_t[:], gn.rearrange("(p t) o -> p (t o)", t=PACK))
         n6_t = load_list("n6_t", n6)
-        w2w = load_words("w2w", w2_words, H)
-        w2s = load_scales("w2s", w2_scales, H, nc.gpsimd, nc.sync)
         n3_t = load_list("n3_t", n3)
         n1_t = load_list("n1_t", n1)
+        w2w = load_words("w2w", w2_words, H)
+        ident = keep.tile([P, P], F32, name="ident")
+        make_identity(nc, ident[:])
+        w2s = load_scales("w2s", w2_scales, H, nc.gpsimd, nc.gpsimd)
         n4_t = load_list("n4_t", n4)
         n5_t = load_list("n5_t", n5)
 
@@ -98,8 +101,6 @@ def tile_picked_skipflowblerp_none_po_kernel(
         xgw = keep.tile([P, S], U32, name="xgw", align_bytes=64)
         nc.vector.tensor_copy(xgs[:], xs[:].indirect(offs_t[:]))
         nc.vector.tensor_copy(xgw[:], xw[:].bitcast(U32).indirect(offs_t[:]))
-        neg_gn = keep.tile([P, PACK], F32, name="neg_gn")
-        nc.vector.tensor_scalar(neg_gn[:], gn_t[:], -1.0, None, ALU.mult)
 
         y_ps = [psum.tile([P, S], F32, name="y_ps%d" % t) for t in range(PACK)]
         h_ps = [psum.tile([P, S], F32, name="h_ps%d" % t) for t in range(PACK)]
@@ -117,8 +118,6 @@ def tile_picked_skipflowblerp_none_po_kernel(
         y = [keep.tile([P, 2 * S], F32, name="y%d" % t) for t in range(PACK)]
         for t in range(PACK):
             nc.gpsimd.memset(y[t][:, S:], 0.0)
-        ident = keep.tile([P, P], F32, name="ident")
-        make_identity(nc, ident[:])
         h = [keep.tile([P, S], F32, name="h%d" % t) for t in range(PACK)]
         hc = [keep.tile([P, S], F32, name="hc%d" % t) for t in range(PACK)]
         zw = keep.tile([P, S], U32, name="zw", align_bytes=64)
@@ -135,7 +134,7 @@ def tile_picked_skipflowblerp_none_po_kernel(
             qg = keep.tile([P, n], F32, name="qg%d_%d" % (lo, t))
             nc.scalar.activation(s[:], y[t][:].indirect(entries(n2_t, lo, hi)), ACT.Sigmoid)
             nc.scalar.activation(sg[:], s[:], ACT.Identity, scale=gn_t[:, t : t + 1])
-            nc.vector.tensor_scalar(qg[:], s[:], neg_gn[:, t : t + 1], gn_t[:, t : t + 1], ALU.mult, ALU.add)
+            nc.scalar.activation(qg[:], sg[:], ACT.Identity, scale=-1.0, bias=gn_t[:, t : t + 1])
             nc.vector.tensor_tensor(b[:, t, lo:hi], y[t][:].indirect(entries(n3_t, lo, hi)), sg[:], ALU.mult)
             nc.vector.tensor_tensor(a[:, t, lo:hi], y[t][:].indirect(entries(n1_t, lo, hi)), qg[:], ALU.mult)
 
@@ -174,7 +173,6 @@ def tile_picked_skipflowblerp_none_po_kernel(
         osc = keep.tile([P, S], U8, name="osc", align_bytes=64)
         out_rows = out_0.rearrange("(p t) j -> p t j", t=PACK)
         parts = {}
-        last = len(OUT_CHUNKS) - 1
 
         def differences(c, t):
             lo, hi = OUT_CHUNKS[c]
@@ -193,9 +191,9 @@ def tile_picked_skipflowblerp_none_po_kernel(
             nc.vector.tensor_tensor(v[:, :fetched, :], d5[:, :fetched, :], y6[:, :fetched, lo:hi], ALU.mult)
             for t in range(fetched, PACK):
                 nc.vector.tensor_tensor(v[:, t, :], y[t][:].indirect(entries(n6_t, lo, hi)), d5[:, t, :], ALU.mult)
-            nc.vector.scalar_tensor_tensor(u[:], d4[:], 1.0 if c == last else 2.0, y_all[:, :, lo:hi], ALU.mult, ALU.mult)
+            nc.vector.scalar_tensor_tensor(u[:], d4[:], 2.0 if c == 0 else 1.0, y_all[:, :, lo:hi], ALU.mult, ALU.mult)
 
-        def sum_on_tensor(c, lo):
+        def sum_on_tensor(c, lo, ob):
             d4, d5, u, v = parts[c]
             block = lo // P
             at = slice(lo - OUT_CHUNKS[c][0], lo - OUT_CHUNKS[c][0] + P)
@@ -210,42 +208,35 @@ def tile_picked_skipflowblerp_none_po_kernel(
                 cols = slice(t * P, (t + 1) * P)
                 nc.tensor.transpose(back_ps[:, cols], turned[:, cols], ident[:])
             o = keep.tile([P, PACK, P], F32, name="o%d" % block)
-            ob = keep.tile([P, P, PACK], BF16, name="ob%d" % block, align_bytes=64)
             nc.scalar.copy(o[:], back_ps[:].rearrange("p (t j) -> p t j", t=PACK))
             nc.sync.dma_start(out_rows[:, :, lo : lo + P], o[:])
-            nc.scalar.copy(ob[:], back_ps[:].rearrange("p (t j) -> p j t", t=PACK))
-            return ob
+            nc.scalar.copy(ob, back_ps[:].rearrange("p (t j) -> p j t", t=PACK))
 
-        def sum_on_vector(c):
-            lo, hi = OUT_CHUNKS[c]
-            d4, d5, u, v = parts[c]
-            o = keep.tile([P, PACK, P], F32, name="o_last")
-            ob = keep.tile([P, P, PACK], BF16, name="ob_last", align_bytes=64)
-            nc.vector.scalar_tensor_tensor(o[:], v[:], 0.5, u[:], ALU.mult, ALU.add)
-            nc.sync.dma_start(out_rows[:, :, lo:hi], o[:])
-            planes(2 * P, rounded[2 * P])
-            nc.vector.tensor_copy(ob[:].rearrange("p (c i) t -> p c t i", i=2), o[:].rearrange("p t (c i) -> p c t i", i=2))
-            return ob
+        def planes(lo, hi, ob):
+            nc.vector.quantize_mx(ow[:, lo:hi].bitcast(FP8X4), osc[:, lo:hi], ob[:].rearrange("p n t -> p (n t)"))
+            nc.sync.dma_start(words_view(out_1)[:, lo:hi], ow[:, lo:hi].bitcast(I32))
 
-        def planes(lo, ob):
-            nc.vector.quantize_mx(ow[:, lo : lo + P].bitcast(FP8X4), osc[:, lo : lo + P], ob[:].rearrange("p n t -> p (n t)"))
-            if lo % (2 * P):
-                nc.sync.dma_start(words_view(out_1)[:, lo - P : lo + P], ow[:, lo - P : lo + P].bitcast(I32))
-
-        rounded = {}
+        half = S // 2
+        rounded = [keep.tile([P, half, PACK], BF16, name="ob%d" % c, align_bytes=64) for c in range(2)]
         for t in range(PACK):
             differences(0, t)
-        for c in range(last):
-            products(c)
-            for lo in range(OUT_CHUNKS[c][0], OUT_CHUNKS[c][1], P):
-                rounded[lo] = sum_on_tensor(c, lo)
-            for t in range(PACK):
-                differences(c + 1, t)
-        planes(0, rounded[0])
-        products(last)
-        planes(P, rounded[P])
-        rounded[3 * P] = sum_on_vector(last)
-        planes(3 * P, rounded[3 * P])
+        products(0)
+        for lo in range(0, half, P):
+            sum_on_tensor(0, lo, rounded[0][:, lo : lo + P, :])
+        for t in range(PACK):
+            differences(1, t)
+        products(1)
+        planes(0, half, rounded[0])
+        d4, d5, u, v = parts[1]
+        o = keep.tile([P, PACK, half], F32, name="o_last")
+        nc.vector.scalar_tensor_tensor(o[:], v[:], 0.5, u[:], ALU.mult, ALU.add)
+        nc.sync.dma_start(out_rows[:, :, half:], o[:])
+        for copy, cols in ((nc.scalar.copy, slice(0, SCALAR_COLS)), (nc.vector.tensor_copy, slice(SCALAR_COLS, half))):
+            copy(
+                rounded[1][:, cols, :].rearrange("p (c i) t -> p c t i", i=2),
+                o[:, :, cols].rearrange("p t (c i) -> p c t i", i=2),
+            )
+        planes(half, S, rounded[1])
         for q in range(4):
             queue = nc.scalar if q % 2 else nc.sync
             queue.dma_start(out_2[0, 4 * q : 4 * q + 4, :].bitcast(I32), osc[32 * q : 32 * q + 4, :].bitcast(I32))

from contextlib import ExitStack

import concourse.mybir as mybir
from concourse.masks import make_identity

F32 = mybir.dt.float32
BF16 = mybir.dt.bfloat16
I32 = mybir.dt.int32
U32 = mybir.dt.uint32
U16 = mybir.dt.uint16
U8 = mybir.dt.uint8
FP8X4 = mybir.dt.float8_e4m3fn_x4
ALU = mybir.AluOpType
ACT = mybir.ActivationFunctionType

P = 128
PACK = 4
T = 2048
S = 512
H = 512
FLOPS = 2 * 2 * 512 * 512 * 512
Z_CHUNKS = [(0, 512)]
OUT_CHUNKS = [(0, 256), (256, 512)]
EARLY = (0, 1)
LATE = (2, 3)
XW_FIRST = 512
SCALAR_COLS = 80


def words_view(dram):
    return dram[0].rearrange("p n t -> p (n t)").bitcast(I32)


def tile_picked_skipflowblerp_none_po_kernel(
    tc, x_words, x_scales, w1_words, w1_scales, gn, w2_words, w2_scales, offs, n1, n2, n3, n4, n5, n6, out_0, out_1, out_2
):
    nc = tc.nc
    with ExitStack() as ctx:
        keep = ctx.enter_context(tc.tile_pool(name="keep", bufs=1))
        psum = ctx.enter_context(tc.psum_pool(name="psum", bufs=1))

        def load_list(name, dram):
            tile = keep.tile([P, S // 16], U16, name=name)
            nc.sync.dma_start(tile[:], dram)
            return tile

        def entries(tile, lo, hi):
            return tile[:, lo // 16 : hi // 16]

        def load_scales(name, dram, width, clear, queue):
            tile = keep.tile([P, width], U8, name=name, tag=name, align_bytes=64)
            clear.memset(tile[:].bitcast(I32), 0)
            for q in range(4):
                queue.dma_start(tile[32 * q : 32 * q + 4, :].bitcast(I32), dram[0, 4 * q : 4 * q + 4, :].bitcast(I32))
            return tile

        def load_words(name, dram, width):
            tile = keep.tile([P, width], I32, name=name, tag=name, align_bytes=64)
            nc.sync.dma_start(tile[:], words_view(dram))
            return tile

        def deal(name, words, scales):
            dealt_words = keep.tile([P, H], U32, name=name + "_dw", tag="w1w", align_bytes=64)
            dealt_scales = keep.tile([P, H], U8, name=name + "_ds", tag="w1s", align_bytes=64)
            nc.vector.tensor_copy(
                dealt_words[:].rearrange("p (t m) -> p m t", t=PACK),
                words[:].bitcast(U32).rearrange("p (m t) -> p m t", t=PACK),
            )
            nc.vector.tensor_copy(
                dealt_scales[:].rearrange("p (t m) -> p t m", t=PACK),
                scales[:].rearrange("p (m t) -> p t m", t=PACK),
            )
            return dealt_words, dealt_scales

        xw = keep.tile([P, T], I32, name="xw", align_bytes=64)
        nc.sync.dma_start(xw[:, :XW_FIRST], words_view(x_words)[:, :XW_FIRST])
        xs = load_scales("xs", x_scales, T, nc.vector, nc.sync)
        offs_t = load_list("offs_t", offs)
        nc.sync.dma_start(xw[:, XW_FIRST:], words_view(x_words)[:, XW_FIRST:])
        warm_in = keep.tile([P, 1], F32, name="warm_in")
        warm_out = keep.tile([P, 1], F32, name="warm_out")
        nc.vector.memset(warm_in[:], 0.0)
        nc.scalar.activation(warm_out[:], warm_in[:], ACT.Sigmoid)

        w1w = load_words("w1w", w1_words, H)
        w1s = load_scales("w1s", w1_scales, H, nc.gpsimd, nc.sync)
        n2_t = load_list("n2_t", n2)
        gn_t = keep.tile([P, PACK], F32, name="gn_t")
        nc.sync.dma_start(gn_t[:], gn.rearrange("(p t) o -> p (t o)", t=PACK))
        n6_t = load_list("n6_t", n6)
        n3_t = load_list("n3_t", n3)
        n1_t = load_list("n1_t", n1)
        w2w = load_words("w2w", w2_words, H)
        ident = keep.tile([P, P], F32, name="ident")
        make_identity(nc, ident[:])
        w2s = load_scales("w2s", w2_scales, H, nc.gpsimd, nc.gpsimd)
        n4_t = load_list("n4_t", n4)
        n5_t = load_list("n5_t", n5)

        xgs = keep.tile([P, S], U8, name="xgs", align_bytes=64)
        xgw = keep.tile([P, S], U32, name="xgw", align_bytes=64)
        nc.vector.tensor_copy(xgs[:], xs[:].indirect(offs_t[:]))
        nc.vector.tensor_copy(xgw[:], xw[:].bitcast(U32).indirect(offs_t[:]))

        y_ps = [psum.tile([P, S], F32, name="y_ps%d" % t) for t in range(PACK)]
        h_ps = [psum.tile([P, S], F32, name="h_ps%d" % t) for t in range(PACK)]
        for t in range(PACK):
            w1dw = keep.tile([P, P], U32, name="w1dw%d" % t, align_bytes=64)
            w1ds = keep.tile([P, P], U8, name="w1ds%d" % t, align_bytes=64)
            nc.vector.tensor_copy(w1dw[:], w1w[:].bitcast(U32)[:, t::PACK])
            nc.vector.tensor_copy(w1ds[:], w1s[:, t::PACK])
            nc.tensor.matmul_mx(
                y_ps[t][:], lhsT=w1dw[:].bitcast(FP8X4), lhsT_scale=w1ds[:],
                rhs=xgw[:].bitcast(FP8X4), rhs_scale=xgs[:], start=True, stop=True,
            )
        w2dw, w2ds = deal("w2", w2w, w2s)

        y = [keep.tile([P, 2 * S], F32, name="y%d" % t) for t in range(PACK)]
        for t in range(PACK):
            nc.gpsimd.memset(y[t][:, S:], 0.0)
        h = [keep.tile([P, S], F32, name="h%d" % t) for t in range(PACK)]
        hc = [keep.tile([P, S], F32, name="hc%d" % t) for t in range(PACK)]
        zw = keep.tile([P, S], U32, name="zw", align_bytes=64)
        zs = keep.tile([P, S], U8, name="zs", align_bytes=64)
        shared = keep.tile([P, len(EARLY) + PACK, S], F32, name="shared")
        y6 = shared[:, :PACK, :]
        a = shared[:, len(EARLY) :, :]
        b = keep.tile([P, PACK, S], F32, name="b", tag="w2w", align_bytes=64)

        def blend(t, lo, hi):
            n = hi - lo
            s = keep.tile([P, n], F32, name="s%d_%d" % (lo, t), tag="s%d_%d" % (lo, t))
            sg = keep.tile([P, n], F32, name="sg%d_%d" % (lo, t), tag="w2s" if t == 1 else "sg%d_%d" % (lo, t), align_bytes=64)
            qg = keep.tile([P, n], F32, name="qg%d_%d" % (lo, t))
            nc.scalar.activation(s[:], y[t][:].indirect(entries(n2_t, lo, hi)), ACT.Sigmoid)
            nc.scalar.activation(sg[:], s[:], ACT.Identity, scale=gn_t[:, t : t + 1])
            nc.scalar.activation(qg[:], sg[:], ACT.Identity, scale=-1.0, bias=gn_t[:, t : t + 1])
            nc.vector.tensor_tensor(b[:, t, lo:hi], y[t][:].indirect(entries(n3_t, lo, hi)), sg[:], ALU.mult)
            nc.vector.tensor_tensor(a[:, t, lo:hi], y[t][:].indirect(entries(n1_t, lo, hi)), qg[:], ALU.mult)

        def second_product(lo, hi):
            zb = keep.tile([P, hi - lo, PACK], BF16, name="zb%d" % lo, align_bytes=64)
            nc.vector.tensor_tensor(
                zb[:].rearrange("p (c i) t -> p c t i", i=2),
                a[:, :, lo:hi].rearrange("p t (c i) -> p c t i", i=2),
                b[:, :, lo:hi].rearrange("p t (c i) -> p c t i", i=2),
                ALU.add,
            )
            nc.vector.quantize_mx(zw[:, lo:hi].bitcast(FP8X4), zs[:, lo:hi], zb[:].rearrange("p n t -> p (n t)"))
            for t in range(PACK):
                cols = slice(t * P, (t + 1) * P)
                nc.tensor.matmul_mx(
                    h_ps[t][:, lo:hi], lhsT=w2dw[:, cols].bitcast(FP8X4), lhsT_scale=w2ds[:, cols],
                    rhs=zw[:, lo:hi].bitcast(FP8X4), rhs_scale=zs[:, lo:hi], start=True, stop=True,
                )

        for t in range(PACK):
            nc.scalar.copy(y[t][:, :S], y_ps[t][:])
            blend(t, 0, S)
        second_product(0, S)
        for t in range(PACK):
            nc.scalar.copy(h[t][:], h_ps[t][:])
            nc.scalar.copy(hc[t][:], h_ps[t][:])
        y_all = keep.tile([P, PACK, S], F32, name="y_all", tag="s0_3")
        for t in range(PACK):
            nc.scalar.copy(y_all[:, t, :], y_ps[t][:])

        fetched = len(EARLY + LATE)
        for t in EARLY + LATE:
            nc.vector.tensor_copy(y6[:, t, :], y[t][:].indirect(n6_t[:]))

        ow = keep.tile([P, S], U32, name="ow", align_bytes=64)
        osc = keep.tile([P, S], U8, name="osc", align_bytes=64)
        out_rows = out_0.rearrange("(p t) j -> p t j", t=PACK)
        parts = {}

        def differences(c, t):
            lo, hi = OUT_CHUNKS[c]
            if t == 0:
                parts[c] = [
                    keep.tile([P, PACK, hi - lo], F32, name="%s_%d" % (nm, c), tag=nm if nm[0] == "d" else "%s_%d" % (nm, c))
                    for nm in ("d4", "d5", "u", "v")
                ]
            d4, d5, u, v = parts[c]
            nc.vector.tensor_tensor(d5[:, t, :], h[t][:].indirect(entries(n5_t, lo, hi)), hc[t][:, lo:hi], ALU.subtract)
            nc.vector.tensor_tensor(d4[:, t, :], h[t][:].indirect(entries(n4_t, lo, hi)), hc[t][:, lo:hi], ALU.subtract)

        def products(c):
            lo, hi = OUT_CHUNKS[c]
            d4, d5, u, v = parts[c]
            nc.vector.tensor_tensor(v[:, :fetched, :], d5[:, :fetched, :], y6[:, :fetched, lo:hi], ALU.mult)
            for t in range(fetched, PACK):
                nc.vector.tensor_tensor(v[:, t, :], y[t][:].indirect(entries(n6_t, lo, hi)), d5[:, t, :], ALU.mult)
            nc.vector.scalar_tensor_tensor(u[:], d4[:], 2.0 if c == 0 else 1.0, y_all[:, :, lo:hi], ALU.mult, ALU.mult)

        def sum_on_tensor(c, lo, ob):
            d4, d5, u, v = parts[c]
            block = lo // P
            at = slice(lo - OUT_CHUNKS[c][0], lo - OUT_CHUNKS[c][0] + P)
            turned_ps, back_ps = y_ps[2 * (block % 2)], y_ps[2 * (block % 2) + 1]
            for t in range(PACK):
                cols = slice(t * P, (t + 1) * P)
                nc.tensor.matmul(turned_ps[:, cols], u[:, t, at], ident[:], is_transpose=True, start=True, stop=False)
                nc.tensor.matmul(turned_ps[:, cols], v[:, t, at], ident[:], is_transpose=True, start=False, stop=True)
            turned = keep.tile([P, S], F32, name="turned%d" % block)
            nc.scalar.activation(turned[:], turned_ps[:], ACT.Copy, scale=0.5)
            for t in range(PACK):
                cols = slice(t * P, (t + 1) * P)
                nc.tensor.transpose(back_ps[:, cols], turned[:, cols], ident[:])
            o = keep.tile([P, PACK, P], F32, name="o%d" % block)
            nc.scalar.copy(o[:], back_ps[:].rearrange("p (t j) -> p t j", t=PACK))
            nc.sync.dma_start(out_rows[:, :, lo : lo + P], o[:])
            nc.scalar.copy(ob, back_ps[:].rearrange("p (t j) -> p j t", t=PACK))

        def planes(lo, hi, ob):
            nc.vector.quantize_mx(ow[:, lo:hi].bitcast(FP8X4), osc[:, lo:hi], ob[:].rearrange("p n t -> p (n t)"))
            nc.sync.dma_start(words_view(out_1)[:, lo:hi], ow[:, lo:hi].bitcast(I32))

        half = S // 2
        rounded = [keep.tile([P, half, PACK], BF16, name="ob%d" % c, align_bytes=64) for c in range(2)]
        for t in range(PACK):
            differences(0, t)
        products(0)
        for lo in range(0, half, P):
            sum_on_tensor(0, lo, rounded[0][:, lo : lo + P, :])
        for t in range(PACK):
            differences(1, t)
        products(1)
        planes(0, half, rounded[0])
        d4, d5, u, v = parts[1]
        o = keep.tile([P, PACK, half], F32, name="o_last")
        nc.vector.scalar_tensor_tensor(o[:], v[:], 0.5, u[:], ALU.mult, ALU.add)
        nc.sync.dma_start(out_rows[:, :, half:], o[:])
        for copy, cols in ((nc.scalar.copy, slice(0, SCALAR_COLS)), (nc.vector.tensor_copy, slice(SCALAR_COLS, half))):
            copy(
                rounded[1][:, cols, :].rearrange("p (c i) t -> p c t i", i=2),
                o[:, :, cols].rearrange("p t (c i) -> p c t i", i=2),
            )
        planes(half, S, rounded[1])
        for q in range(4):
            queue = nc.scalar if q % 2 else nc.sync
            queue.dma_start(out_2[0, 4 * q : 4 * q + 4, :].bitcast(I32), osc[32 * q : 32 * q + 4, :].bitcast(I32))
